import numpy as np
import ml_dtypes


def mxq(x, axis, fmt="e4m3"):
    dtype, down = {"e4m3": (ml_dtypes.float8_e4m3fn, 7), "e5m2": (ml_dtypes.float8_e5m2, 14)}[fmt]
    v = np.moveaxis(np.asarray(x, np.float32).astype(ml_dtypes.bfloat16).astype(np.float64), axis, -1)
    blocks = v.reshape(v.shape[:-1] + (-1, 32))
    amax = np.abs(blocks).max(-1, keepdims=True)
    byte = np.maximum(np.where(amax > 0, np.frexp(amax)[1] - 1 + 127, 0) - down, 1)
    scale = np.exp2(byte - 127.0)
    codes = (blocks / scale).astype(np.float32).astype(dtype).astype(np.float64)
    return np.moveaxis((codes * scale).reshape(v.shape), -1, axis)


WIDE = False


def mx_kscale(k):
    if not WIDE:
        return np.ones(k)
    levels = np.array([10, -10, 5, -5, 0])
    if k % 512:
        return np.exp2(np.random.permutation(np.resize(levels, k // 32))).repeat(32)
    a = np.empty((k // 512, 16))
    for p in range(k // 512):
        a[p, :8] = np.random.permutation(np.resize(levels, 8))
        for g in range(8):
            far = levels[np.abs(levels - a[p, g]) >= 10]
            a[p, g + 8] = far[np.random.randint(len(far))]
    return np.exp2(a.ravel()).repeat(32)


def f64(x):
    return np.asarray(x).astype(np.float64)


def striped(idx):
    return np.tile(idx.reshape(-1, 16).T, (8, 1)).astype(np.uint16)


def unstriped(offs):
    return offs[:16].T.reshape(-1).astype(np.int64)


E2M1 = np.array([0.0, 0.5, 1.0, 1.5, 2.0, 3.0, 4.0, 6.0, -0.0, -0.5, -1.0, -1.5, -2.0, -3.0, -4.0, -6.0])


def pack_weight(w, fmt):
    k, n = w.shape
    w = f64(np.asarray(w, np.float32).astype(ml_dtypes.bfloat16)).reshape(k // 32, 32, n)
    amax = np.abs(w).max(1)
    if fmt == "e4m3":
        byte = np.frexp(amax)[1] - 1 + 127 - 7
    else:
        mant, ex = np.frexp(amax / 6.0)
        byte = np.where(mant > 0.5, ex, ex - 1) + 127
    byte = np.clip(np.where(amax > 0, byte, 1), 1, 254)
    scaled = (w * np.exp2(127.0 - byte)[:, None, :]).reshape(k, n).astype(np.float32)
    by_word = np.ascontiguousarray(scaled.reshape(k // 512, 128, 4, n).transpose(0, 1, 3, 2))
    if fmt == "e4m3":
        words = by_word.astype(ml_dtypes.float8_e4m3fn).view(np.uint8)
    else:
        c = by_word.astype(ml_dtypes.float4_e2m1fn).view(np.uint8) & 0xF
        words = (c[..., 0::2] | (c[..., 1::2] << 4)).reshape(k // 512, 128, 2 * n)
    return np.ascontiguousarray(words), np.ascontiguousarray(byte.astype(np.uint8).reshape(k // 512, 16, n))


def unpack_weight(words, scales, fmt):
    g, _, n = scales.shape
    words = np.ascontiguousarray(words).reshape(g, 128, n, -1)
    if fmt == "e4m3":
        vals = words.view(ml_dtypes.float8_e4m3fn).astype(np.float64)
    else:
        nib = np.empty((g, 128, n, 4), np.uint8)
        nib[..., 0::2] = words & 0xF
        nib[..., 1::2] = words >> 4
        vals = E2M1[nib]
    vals = vals * np.repeat(np.exp2(scales.astype(np.float64) - 127.0), 8, axis=1)[..., None]
    return vals.transpose(0, 1, 3, 2).reshape(g * 512, n)


def gelu(v):
    return 0.5 * v * (1.0 + np.tanh(np.sqrt(2.0 / np.pi) * (v + 0.044715 * v**3)))


def striped8(idx):
    return np.concatenate([v.reshape(-1, 16).T for v in idx]).astype(np.uint16)


def unstriped8(offs):
    return np.stack([offs[16 * g:16 * g + 16].T.reshape(-1) for g in range(8)]).astype(np.int64)


def runs(v, idx8):
    k = np.arange(v.shape[0])
    return v[k[:, None], idx8[k % 512 // 64]]


def bf(x):
    return np.asarray(x, np.float32).astype(ml_dtypes.bfloat16)


def planes(Y):
    n, m = Y.shape
    b = f64(bf(Y)).reshape(n // 32, 32, m)
    amax = np.abs(b).max(1)
    byte = np.clip(np.where(amax > 0, np.frexp(amax)[1] - 1 + 127 - 7, 1), 1, 254)
    codes = (b * np.exp2(127.0 - byte)[:, None, :]).reshape(n, m).astype(np.float32).astype(ml_dtypes.float8_e4m3fn).view(np.uint8)
    words = codes.reshape(n // 512, 128, 4, m).transpose(0, 1, 3, 2)
    return np.ascontiguousarray(words), np.ascontiguousarray(byte.astype(np.uint8).reshape(n // 512, 16, m))


K, H, N, T, S, P = 1024, 1024, 512, 2048, 1024, 512


def setup_inputs():
    n = np.random.standard_normal
    s = mx_kscale(K)[:, None]
    u = mx_kscale(H)[:, None]
    d = {}
    d["tab_words"], d["tab_scales"] = pack_weight(n((K, T)) * s, "e4m3")
    d["offs"] = striped8(np.stack([np.random.permutation(T)[:S] for _ in range(8)]))
    d["pos1"] = striped(np.random.permutation(S)[:P])
    d["pos2"] = striped(np.random.permutation(S)[:P])
    d["w1"] = (n((K, H)) / K ** 0.5 / s * u.T).astype(np.float32)
    d["w4_words"], d["w4_scales"] = pack_weight(n((K, H)) / K ** 0.5 / s * u.T, "e2m1")
    d["low"] = (0.6 * n(H) * u[:, 0]).astype(np.float32)
    d["w2"] = (n((H, N)) / H ** 0.5 / u * np.exp(0.8 * n(N))[None, :]).astype(np.float32)
    return d


def reference(tab_words, tab_scales, offs, pos1, pos2, w1, w4_words, w4_scales, low, w2):
    v = runs(unpack_weight(tab_words, tab_scales, "e4m3"), unstriped8(offs))
    w4 = unpack_weight(w4_words, w4_scales, "e2m1")
    a = mxq(f64(w1), 0, "e4m3").T @ v
    b = w4.T @ v
    h = np.abs(a) - np.abs(b)
    port = h[:, unstriped(pos1)]
    starboard = h[:, unstriped(pos2)]
    x = np.maximum(starboard, f64(low)[:, None]) + port
    y = mxq(f64(w2), 0, "e4m3").T @ mxq(x, 0, "e4m3")
    words, scales = planes(y)
    return y, words, scales

@@ -1,0 +1,318 @@
+from contextlib import ExitStack
+
+import concourse.mybir as mybir
+from concourse.masks import make_identity
+
+K, H, N, T, S, M = 1024, 1024, 512, 2048, 1024, 512
+FLOPS = 2 * 2 * K * H * S + 2 * H * N * M
+
+F32 = mybir.dt.float32
+BF16 = mybir.dt.bfloat16
+I32 = mybir.dt.int32
+U32 = mybir.dt.uint32
+U16 = mybir.dt.uint16
+U8 = mybir.dt.uint8
+FP8X4 = mybir.dt.float8_e4m3fn_x4
+FP4X4 = mybir.dt.float4_e2m1fn_x4
+ALU = mybir.AluOpType
+ACT = mybir.ActivationFunctionType
+
+P = 128
+BANK = 512
+HALF = M // 2
+
+
+def tile_list_trawl_geometry_features_kernel(
+    tc, tab_words, tab_scales, offs, pos1, pos2, w1, w4_words, w4_scales, low, w2, out_0, out_1, out_2
+):
+    nc = tc.nc
+    with ExitStack() as ctx:
+        keep = ctx.enter_context(tc.tile_pool(name="keep", bufs=1))
+        ring = ctx.enter_context(tc.tile_pool(name="ring", bufs=2))
+        psum = ctx.enter_context(tc.psum_pool(name="psum", bufs=4))
+
+        def kept(shape, dtype, name, tag=None):
+            return keep.tile(shape, dtype, name=name, tag=tag or name, align_bytes=64)
+
+        offs_t = kept([P, S // 16], U16, "offs_t")
+        pos1_t = kept([P, M // 16], U16, "pos1_t")
+        pos2_t = kept([P, M // 16], U16, "pos2_t")
+        tab_s = kept([P, T], U8, "tab_s", "stage_x")
+        tab_w = [kept([P, T], U32, "tab_w0", "stage_y"), kept([P, T], U32, "tab_w1", "stage_z")]
+        w4_raw = kept([P, 2, H // 2], I32, "w4_raw")
+        w4s_raw = kept([P, 2, H // 4], I32, "w4s_raw")
+        v_s = kept([P, 2 * S], U8, "v_s")
+        low_rows = kept([P, P], F32, "low_rows")
+        ident = kept([P, P], F32, "ident")
+
+        nc.vector.memset(tab_s[:].bitcast(I32), 0)
+        nc.vector.memset(w4s_raw[:], 0)
+        nc.vector.memset(low_rows[:], 0.0)
+        nc.vector.memset(v_s[:].bitcast(I32), 0)
+
+        nc.sync.dma_start(offs_t[:], offs)
+        nc.scalar.dma_start(tab_s[0:P:4, :].bitcast(I32), tab_scales.rearrange("a q t -> q a t").bitcast(I32))
+        nc.sync.dma_start(tab_w[0][:].bitcast(I32), tab_words[0].rearrange("p t i -> p (t i)").bitcast(I32))
+        nc.sync.dma_start(tab_w[1][:].bitcast(I32), tab_words[1].rearrange("p t i -> p (t i)").bitcast(I32))
+        nc.sync.dma_start(w4_raw[:], w4_words.rearrange("a p c -> p a c").bitcast(I32))
+        nc.sync.dma_start(pos1_t[:], pos1)
+        nc.sync.dma_start(pos2_t[:], pos2)
+        for d in range(4):
+            nc.gpsimd.dma_start(
+                w4s_raw[32 * d : 32 * d + 4, :, :],
+                w4_scales[:, 4 * d : 4 * d + 4, :].rearrange("a r c -> r a c").bitcast(I32),
+            )
+        low_src = low.rearrange("(b m t i) -> b t m i", b=2, t=4, i=8)
+        for b in range(2):
+            nc.gpsimd.dma_start(low_rows[4 * b : 4 * b + 4, :].rearrange("t (m i) -> t m i", i=8), low_src[b])
+        make_identity(nc, ident[:])
+        low_ps = psum.tile([P, BANK], F32, name="low_ps", tag="bank_a")
+        nc.tensor.transpose(low_ps[:, 0:P], low_rows[:], ident[:])
+        low_c = kept([P, 8], F32, "low_c")
+        nc.scalar.activation(low_c[:], low_ps[:, 0:8], ACT.Copy)
+
+        picked_s = kept([P, S], U8, "picked_s")
+        nc.vector.tensor_copy(picked_s[:], tab_s[:].indirect(offs_t[:]))
+        for d in range(4):
+            nc.scalar.dma_start(
+                v_s[32 * d : 32 * d + 4, :].bitcast(I32).rearrange("r (a c) -> r a c", a=2),
+                picked_s[32 * d : 32 * d + 32 : 4, :].bitcast(I32),
+            )
+        w1_raw = {}
+
+        def load_w1(b, a, tag):
+            raw = kept([P, 4, BANK], F32, "w1_raw%d%d" % (b, a), tag)
+            rows = w1[512 * a : 512 * a + 512, 512 * b : 512 * b + 512]
+            nc.sync.dma_start(raw[:], rows.rearrange("(p j) c -> p j c", j=4))
+            w1_raw[b, a] = raw
+
+        load_w1(0, 0, "stage_x")
+        v_w = []
+        for a in range(2):
+            words = kept([P, S], U32, "v_w%d" % a)
+            nc.vector.tensor_copy(words[:], tab_w[a][:].indirect(offs_t[:]))
+            v_w.append(words)
+            load_w1(a, 1 - a, "stage_y" if a == 0 else "stage_z")
+
+        w4_w, w4_s = {}, {}
+
+        def deal_w4(b):
+            words = kept([P, 2 * H], U8, "w4_w%d" % b)
+            nc.vector.tensor_copy(
+                words[:].bitcast(I32).rearrange("p (a t m e) -> p a t m e", a=2, t=4, e=4),
+                w4_raw[:, :, 256 * b : 256 * b + 256].rearrange("p a (m t e) -> p a t m e", t=4, e=4),
+            )
+            scales = kept([P, H], U8, "w4_s%d" % b)
+            nc.vector.tensor_copy(
+                scales[:].bitcast(I32).rearrange("p (a t m e) -> p a t m e", a=2, t=4, e=2),
+                w4s_raw[:, :, 128 * b : 128 * b + 128].rearrange("p a (m t e) -> p a t m e", t=4, e=2),
+            )
+            w4_w[b], w4_s[b] = words, scales
+
+        def copy_on(engine, out, in_):
+            if engine == "vector":
+                nc.vector.tensor_copy(out, in_)
+            else:
+                nc.scalar.copy(out, in_)
+
+        w1_bf, w1_q = {}, {}
+
+        def round_w1(b, a, t0, count, engine):
+            tile_ = kept([P, count * 512], BF16, "w1_bf%d%d%d" % (b, a, t0))
+            src = w1_raw[b, a][:].rearrange("p j (m t h l) -> p t m h j l", t=4, h=2, l=4)
+            for u in range(count):
+                dst = tile_[:, 512 * u : 512 * u + 512].rearrange("p (m h l j) -> p m h j l", h=2, l=4, j=4)
+                copy_on(engine, dst, src[:, t0 + u])
+            w1_bf[b, a, t0] = (tile_, count)
+
+        def quantize(src, width, name):
+            codes = kept([P, width], U32, name + "_w")
+            scales = kept([P, width], U8, name + "_s")
+            nc.vector.quantize_mx(out=codes[:].bitcast(FP8X4), scales=scales[:], in_=src)
+            return codes, scales
+
+        def quantize_w1(b, a, t0):
+            tile_, count = w1_bf[b, a, t0]
+            codes, scales = quantize(tile_[:], count * P, "w1_q%d%d%d" % (b, a, t0))
+            for u in range(count):
+                w1_q[b, a, t0 + u] = (codes[:, P * u : P * u + P], scales[:, P * u : P * u + P])
+
+        size_a, size_b = {}, {}
+
+        def response(b, t, which):
+            size = ring.tile([P, S], F32, name="size_" + which, bufs=3)
+            for half in range(2):
+                acc = psum.tile([P, BANK], F32, name="acc", tag="bank_" + which)
+                cols = slice(BANK * half, BANK * half + BANK)
+                for a in range(2):
+                    if which == "a":
+                        codes, scales = w1_q[b, a, t]
+                        lhs = codes.bitcast(FP8X4)
+                    else:
+                        lhs = w4_w[b][:, 1024 * a + 256 * t : 1024 * a + 256 * t + 256].bitcast(FP4X4)
+                        scales = w4_s[b][:, 512 * a + P * t : 512 * a + P * t + P]
+                    nc.tensor.matmul_mx(
+                        out=acc[:],
+                        lhsT=lhs,
+                        lhsT_scale=scales,
+                        rhs=v_w[a][:, cols].bitcast(FP8X4),
+                        rhs_scale=v_s[:, S * a + BANK * half : S * a + BANK * half + BANK],
+                        start=(a == 0),
+                        stop=(a == 1),
+                    )
+                nc.scalar.activation(size[:, cols], acc[:], ACT.Abs)
+            (size_a if which == "a" else size_b)[b, t] = size
+
+        h_t = {}
+
+        def difference(b, t):
+            h = ring.tile([P, S], F32, name="h", bufs=5)
+            nc.vector.tensor_tensor(h[:], size_a[b, t][:], size_b[b, t][:], ALU.subtract)
+            h_t[b, t] = h
+
+        def pair_up(b, t, m0, width, x_rows):
+            port = ring.tile([P, width], F32, name="port")
+            starboard = ring.tile([P, width], F32, name="starboard")
+            cols = slice(m0 // 16, (m0 + width) // 16)
+            nc.vector.tensor_copy(starboard[:], h_t[b, t][:].indirect(pos2_t[:, cols]))
+            nc.vector.tensor_copy(port[:], h_t[b, t][:].indirect(pos1_t[:, cols]))
+            nc.vector.scalar_tensor_tensor(
+                x_rows[:, t, :], starboard[:], low_c[:, 4 * b + t : 4 * b + t + 1], port[:], ALU.max, ALU.add
+            )
+
+        def interleave(engine, rows, width, name):
+            woven = kept([P, 4 * width], BF16, name)
+            copy_on(
+                engine,
+                woven[:].rearrange("p (c l t) -> p c t l", l=4, t=4),
+                rows.rearrange("p t (c l) -> p c t l", l=4),
+            )
+            return woven
+
+        w2_raw, w2_bf, w2_q = {}, {}, {}
+
+        def load_w2(b, tag):
+            raw = kept([P, 4, N], F32, "w2_raw%d" % b, tag)
+            src = w2[512 * b : 512 * b + 512, :].rearrange("(m t i) n -> t m i n", t=4, i=8)
+            for t in range(4):
+                nc.sync.dma_start(raw[:, t, :], src[t])
+            w2_raw[b] = raw
+
+        def round_w2(b):
+            tile_ = kept([P, 4 * N], BF16, "w2_bf%d" % b)
+            dst = tile_[:].rearrange("p (s q t) -> p q t s", s=4, t=4)
+            src = w2_raw[b][:].rearrange("p t (q s) -> p q t s", s=4)
+            for u in range(4):
+                nc.scalar.copy(dst[:, 32 * u : 32 * u + 32], src[:, 32 * u : 32 * u + 32])
+            w2_bf[b] = tile_
+
+        def quantize_w2(b):
+            w2_q[b] = quantize(w2_bf[b][:], N, "w2_q%d" % b)
+
+        deal_w4(0)
+        response(0, 0, "b")
+        round_w1(0, 0, 0, 4, "vector")
+        quantize_w1(0, 0, 0)
+        load_w1(1, 1, "stage_x")
+        round_w1(0, 1, 0, 1, "vector")
+        round_w1(0, 1, 1, 1, "vector")
+        quantize_w1(0, 1, 0)
+        round_w1(0, 1, 2, 2, "vector")
+        quantize_w1(0, 1, 1)
+        quantize_w1(0, 1, 2)
+        load_w2(0, "stage_y")
+        x_rows0 = kept([P, 4, M], BF16, "x_rows0")
+        response(0, 0, "a")
+        response(0, 1, "b")
+        response(0, 2, "b")
+        response(0, 1, "a")
+        difference(0, 0)
+        pair_up(0, 0, 0, M, x_rows0)
+        deal_w4(1)
+        round_w1(1, 0, 0, 4, "scalar")
+        load_w2(1, "stage_z")
+        difference(0, 1)
+        pair_up(0, 1, 0, M, x_rows0)
+        quantize_w1(1, 0, 0)
+        response(0, 2, "a")
+        response(0, 3, "b")
+        round_w1(1, 1, 0, 4, "scalar")
+        difference(0, 2)
+        pair_up(0, 2, 0, M, x_rows0)
+        quantize_w1(1, 1, 0)
+        response(0, 3, "a")
+        response(1, 0, "b")
+        round_w2(0)
+        difference(0, 3)
+        pair_up(0, 3, 0, M, x_rows0)
+
+        x_rows1 = [kept([P, 4, HALF], BF16, "x_rows1%d" % u) for u in range(2)]
+        response(1, 0, "a")
+        response(1, 1, "b")
+        response(1, 1, "a")
+        x_bf0 = interleave("scalar", x_rows0[:], M, "x_bf0")
+        difference(1, 0)
+        pair_up(1, 0, 0, HALF, x_rows1[0])
+        quantize_w2(0)
+        response(1, 2, "b")
+        response(1, 2, "a")
+        difference(1, 1)
+        pair_up(1, 1, 0, HALF, x_rows1[0])
+        x_q0 = quantize(x_bf0[:], M, "x_q0")
+        response(1, 3, "b")
+        response(1, 3, "a")
+        round_w2(1)
+        difference(1, 2)
+        pair_up(1, 2, 0, HALF, x_rows1[0])
+        difference(1, 3)
+        pair_up(1, 3, 0, HALF, x_rows1[0])
+        quantize_w2(1)
+
+        y_w = kept([P, M], U32, "y_w")
+        y_s = kept([P, M], U8, "y_s")
+        y_out = out_0.rearrange("(q s) m -> q s m", s=4)
+        words_out = out_1[0].rearrange("p m t -> p (m t)").bitcast(I32)
+
+        def features(u, x_q1, engines):
+            cols = slice(HALF * u, HALF * u + HALF)
+            y = kept([P, 4, HALF], F32, "y%d" % u)
+            for s in range(4):
+                acc = psum.tile([P, BANK], F32, name="acc", tag="bank_a" if u == 0 else "bank_b")
+                for b in range(2):
+                    codes, scales = w2_q[b]
+                    x_w, x_s = (x_q0[0][:, cols], x_q0[1][:, cols]) if b == 0 else (x_q1[0][:], x_q1[1][:])
+                    nc.tensor.matmul_mx(
+                        out=acc[:, 0:HALF],
+                        lhsT=codes[:, P * s : P * s + P].bitcast(FP8X4),
+                        lhsT_scale=scales[:, P * s : P * s + P],
+                        rhs=x_w.bitcast(FP8X4),
+                        rhs_scale=x_s,
+                        start=(b == 0),
+                        stop=(b == 1),
+                    )
+                copy_on(engines[s % 2], y[:, s, :], acc[:, 0:HALF])
+            nc.sync.dma_start(y_out[:, :, cols], y[:])
+            return y
+
+        def planes(u, y_bf):
+            cols = slice(HALF * u, HALF * u + HALF)
+            nc.vector.quantize_mx(out=y_w[:, cols].bitcast(FP8X4), scales=y_s[:, cols], in_=y_bf[:])
+            nc.sync.dma_start(words_out[:, cols], y_w[:, cols].bitcast(I32))
+
+        x_bf10 = interleave("scalar", x_rows1[0][:], HALF, "x_bf10")
+        pair_up(1, 0, HALF, HALF, x_rows1[1])
+        x_q10 = quantize(x_bf10[:], HALF, "x_q10")
+        y0 = features(0, x_q10, ("scalar", "scalar"))
+        y_bf0 = interleave("scalar", y0[:], HALF, "y_bf0")
+        pair_up(1, 1, HALF, HALF, x_rows1[1])
+        pair_up(1, 2, HALF, HALF, x_rows1[1])
+        pair_up(1, 3, HALF, HALF, x_rows1[1])
+        x_bf11 = interleave("vector", x_rows1[1][:], HALF, "x_bf11")
+        planes(0, y_bf0)
+        x_q11 = quantize(x_bf11[:], HALF, "x_q11")
+        y1 = features(1, x_q11, ("scalar", "vector"))
+        y_bf1 = interleave("vector", y1[:], HALF, "y_bf1")
+        planes(1, y_bf1)
+        for d in range(4):
+            queue = nc.scalar if d % 2 else nc.sync
+            queue.dma_start(out_2[0, 4 * d : 4 * d + 4, :].bitcast(I32), y_s[32 * d : 32 * d + 4, :].bitcast(I32))

@@ -39,46 +39,28 @@ def tile_list_trawl_geometry_features_kernel(
         pos2_t = kept([P, M // 16], U16, "pos2_t")
         tab_s = kept([P, T], U8, "tab_s", "stage_x")
         tab_w = [kept([P, T], U32, "tab_w0", "stage_y"), kept([P, T], U32, "tab_w1", "stage_z")]
-        w4_raw = kept([P, 2, H // 2], I32, "w4_raw")
         w4s_raw = kept([P, 2, H // 4], I32, "w4s_raw")
         v_s = kept([P, 2 * S], U8, "v_s")
         low_rows = kept([P, P], F32, "low_rows")
         ident = kept([P, P], F32, "ident")
 
-        nc.vector.memset(tab_s[:].bitcast(I32), 0)
+        nc.gpsimd.memset(tab_s[:].bitcast(I32), 0)
+        nc.gpsimd.memset(low_rows[:], 0.0)
         nc.vector.memset(w4s_raw[:], 0)
-        nc.vector.memset(low_rows[:], 0.0)
         nc.vector.memset(v_s[:].bitcast(I32), 0)
 
         nc.sync.dma_start(offs_t[:], offs)
-        nc.scalar.dma_start(tab_s[0:P:4, :].bitcast(I32), tab_scales.rearrange("a q t -> q a t").bitcast(I32))
-        nc.sync.dma_start(tab_w[0][:].bitcast(I32), tab_words[0].rearrange("p t i -> p (t i)").bitcast(I32))
-        nc.sync.dma_start(tab_w[1][:].bitcast(I32), tab_words[1].rearrange("p t i -> p (t i)").bitcast(I32))
-        nc.sync.dma_start(w4_raw[:], w4_words.rearrange("a p c -> p a c").bitcast(I32))
         nc.sync.dma_start(pos1_t[:], pos1)
         nc.sync.dma_start(pos2_t[:], pos2)
-        for d in range(4):
-            nc.gpsimd.dma_start(
-                w4s_raw[32 * d : 32 * d + 4, :, :],
-                w4_scales[:, 4 * d : 4 * d + 4, :].rearrange("a r c -> r a c").bitcast(I32),
-            )
-        low_src = low.rearrange("(b m t i) -> b t m i", b=2, t=4, i=8)
-        for b in range(2):
-            nc.gpsimd.dma_start(low_rows[4 * b : 4 * b + 4, :].rearrange("t (m i) -> t m i", i=8), low_src[b])
-        make_identity(nc, ident[:])
-        low_ps = psum.tile([P, BANK], F32, name="low_ps", tag="bank_a")
-        nc.tensor.transpose(low_ps[:, 0:P], low_rows[:], ident[:])
-        low_c = kept([P, 8], F32, "low_c")
-        nc.scalar.activation(low_c[:], low_ps[:, 0:8], ACT.Copy)
+        nc.sync.dma_start(tab_s[0:P:4, :].bitcast(I32), tab_scales.rearrange("a q t -> q a t").bitcast(I32))
+        nc.sync.dma_start(tab_w[0][:].bitcast(I32), tab_words[0].rearrange("p t i -> p (t i)").bitcast(I32))
+        w4_raw, w1_raw = {}, {}
 
-        picked_s = kept([P, S], U8, "picked_s")
-        nc.vector.tensor_copy(picked_s[:], tab_s[:].indirect(offs_t[:]))
-        for d in range(4):
-            nc.scalar.dma_start(
-                v_s[32 * d : 32 * d + 4, :].bitcast(I32).rearrange("r (a c) -> r a c", a=2),
-                picked_s[32 * d : 32 * d + 32 : 4, :].bitcast(I32),
-            )
-        w1_raw = {}
+        def load_w4(b, tag):
+            raw = kept([P, 2, H // 4], I32, "w4_raw%d" % b, tag)
+            src = w4_words.rearrange("a p c -> p a c")[:, :, 1024 * b : 1024 * b + 1024]
+            nc.sync.dma_start(raw[:], src.bitcast(I32))
+            w4_raw[b] = raw
 
         def load_w1(b, a, tag):
             raw = kept([P, 4, BANK], F32, "w1_raw%d%d" % (b, a), tag)
@@ -86,13 +68,36 @@ def tile_list_trawl_geometry_features_kernel(
             nc.sync.dma_start(raw[:], rows.rearrange("(p j) c -> p j c", j=4))
             w1_raw[b, a] = raw
 
+        load_w4(0, "w4_raw0")
+        nc.sync.dma_start(tab_w[1][:].bitcast(I32), tab_words[1].rearrange("p t i -> p (t i)").bitcast(I32))
+        low_src = low.rearrange("(b m t i) -> b t m i", b=2, t=4, i=8)
+        for b in range(2):
+            nc.gpsimd.dma_start(low_rows[4 * b : 4 * b + 4, :].rearrange("t (m i) -> t m i", i=8), low_src[b])
+        make_identity(nc, ident[:])
+        for d in range(4):
+            nc.gpsimd.dma_start(
+                w4s_raw[32 * d : 32 * d + 4, :, :],
+                w4_scales[:, 4 * d : 4 * d + 4, :].rearrange("a r c -> r a c").bitcast(I32),
+            )
+        low_ps = psum.tile([P, BANK], F32, name="low_ps", tag="bank_a")
+        nc.tensor.transpose(low_ps[:, 0:P], low_rows[:], ident[:])
+        low_c = kept([P, 8], F32, "low_c")
+        nc.scalar.activation(low_c[:], low_ps[:, 0:8], ACT.Copy)
+
+        picked_s = kept([P, S], U8, "picked_s", "stage_w")
+        nc.vector.tensor_copy(picked_s[:], tab_s[:].indirect(offs_t[:]))
+        for d in range(4):
+            nc.sync.dma_start(
+                v_s[32 * d : 32 * d + 4, :].bitcast(I32).rearrange("r (a c) -> r a c", a=2),
+                picked_s[32 * d : 32 * d + 32 : 4, :].bitcast(I32),
+            )
         load_w1(0, 0, "stage_x")
         v_w = []
-        for a in range(2):
+
+        def pick_words(a):
             words = kept([P, S], U32, "v_w%d" % a)
             nc.vector.tensor_copy(words[:], tab_w[a][:].indirect(offs_t[:]))
             v_w.append(words)
-            load_w1(a, 1 - a, "stage_y" if a == 0 else "stage_z")
 
         w4_w, w4_s = {}, {}
 
@@ -100,7 +105,7 @@ def tile_list_trawl_geometry_features_kernel(
             words = kept([P, 2 * H], U8, "w4_w%d" % b)
             nc.vector.tensor_copy(
                 words[:].bitcast(I32).rearrange("p (a t m e) -> p a t m e", a=2, t=4, e=4),
-                w4_raw[:, :, 256 * b : 256 * b + 256].rearrange("p a (m t e) -> p a t m e", t=4, e=4),
+                w4_raw[b][:].rearrange("p a (m t e) -> p a t m e", t=4, e=4),
             )
             scales = kept([P, H], U8, "w4_s%d" % b)
             nc.vector.tensor_copy(
@@ -139,35 +144,46 @@ def tile_list_trawl_geometry_features_kernel(
 
         size_a, size_b = {}, {}
 
-        def response(b, t, which):
+        banks = {}
+
+        def one_pass(b, t, which, a):
+            for half in range(2):
+                if a == 0:
+                    banks[b, t, which, half] = psum.tile([P, BANK], F32, name="acc", tag="bank_" + which)
+                if which == "a":
+                    codes, scales = w1_q[b, a, t]
+                    lhs = codes.bitcast(FP8X4)
+                else:
+                    lhs = w4_w[b][:, 1024 * a + 256 * t : 1024 * a + 256 * t + 256].bitcast(FP4X4)
+                    scales = w4_s[b][:, 512 * a + P * t : 512 * a + P * t + P]
+                nc.tensor.matmul_mx(
+                    out=banks[b, t, which, half][:],
+                    lhsT=lhs,
+                    lhsT_scale=scales,
+                    rhs=v_w[a][:, BANK * half : BANK * half + BANK].bitcast(FP8X4),
+                    rhs_scale=v_s[:, S * a + BANK * half : S * a + BANK * half + BANK],
+                    start=(a == 0),
+                    stop=(a == 1),
+                )
+
+        def take_size(b, t, which):
             size = ring.tile([P, S], F32, name="size_" + which, bufs=3)
             for half in range(2):
-                acc = psum.tile([P, BANK], F32, name="acc", tag="bank_" + which)
-                cols = slice(BANK * half, BANK * half + BANK)
-                for a in range(2):
-                    if which == "a":
-                        codes, scales = w1_q[b, a, t]
-                        lhs = codes.bitcast(FP8X4)
-                    else:
-                        lhs = w4_w[b][:, 1024 * a + 256 * t : 1024 * a + 256 * t + 256].bitcast(FP4X4)
-                        scales = w4_s[b][:, 512 * a + P * t : 512 * a + P * t + P]
-                    nc.tensor.matmul_mx(
-                        out=acc[:],
-                        lhsT=lhs,
-                        lhsT_scale=scales,
-                        rhs=v_w[a][:, cols].bitcast(FP8X4),
-                        rhs_scale=v_s[:, S * a + BANK * half : S * a + BANK * half + BANK],
-                        start=(a == 0),
-                        stop=(a == 1),
-                    )
-                nc.scalar.activation(size[:, cols], acc[:], ACT.Abs)
+                nc.scalar.activation(size[:, BANK * half : BANK * half + BANK], banks[b, t, which, half][:], ACT.Abs)
             (size_a if which == "a" else size_b)[b, t] = size
+
+        def response(b, t, which):
+            one_pass(b, t, which, 0)
+            one_pass(b, t, which, 1)
+            take_size(b, t, which)
 
         h_t = {}
 
-        def difference(b, t):
-            h = ring.tile([P, S], F32, name="h", bufs=5)
-            nc.vector.tensor_tensor(h[:], size_a[b, t][:], size_b[b, t][:], ALU.subtract)
+        def difference(b, t, engine):
+            h = ring.tile([P, S], F32, name="h", bufs=6)
+            for half in range(2):
+                cols = slice(BANK * half, BANK * half + BANK)
+                engine.tensor_tensor(h[:, cols], size_a[b, t][:, cols], size_b[b, t][:, cols], ALU.subtract)
             h_t[b, t] = h
 
         def pair_up(b, t, m0, width, x_rows):
@@ -209,64 +225,71 @@ def tile_list_trawl_geometry_features_kernel(
         def quantize_w2(b):
             w2_q[b] = quantize(w2_bf[b][:], N, "w2_q%d" % b)
 
+        pick_words(0)
+        load_w1(0, 1, "stage_y")
+        load_w4(1, "stage_w")
         deal_w4(0)
-        response(0, 0, "b")
-        round_w1(0, 0, 0, 4, "vector")
+        one_pass(0, 0, "b", 0)
+        one_pass(0, 1, "b", 0)
+        pick_words(1)
+        load_w1(1, 0, "stage_z")
+        round_w1(0, 0, 0, 2, "scalar")
+        round_w1(0, 0, 2, 2, "scalar")
+        one_pass(0, 0, "b", 1)
+        take_size(0, 0, "b")
         quantize_w1(0, 0, 0)
+        one_pass(0, 0, "a", 0)
         load_w1(1, 1, "stage_x")
         round_w1(0, 1, 0, 1, "vector")
         round_w1(0, 1, 1, 1, "vector")
         quantize_w1(0, 1, 0)
+        one_pass(0, 0, "a", 1)
+        take_size(0, 0, "a")
         round_w1(0, 1, 2, 2, "vector")
         quantize_w1(0, 1, 1)
+        quantize_w1(0, 0, 2)
         quantize_w1(0, 1, 2)
         load_w2(0, "stage_y")
         x_rows0 = kept([P, 4, M], BF16, "x_rows0")
-        response(0, 0, "a")
-        response(0, 1, "b")
-        response(0, 2, "b")
+        one_pass(0, 1, "b", 1)
+        take_size(0, 1, "b")
         response(0, 1, "a")
-        difference(0, 0)
+        difference(0, 0, nc.vector)
+        difference(0, 1, nc.gpsimd)
         pair_up(0, 0, 0, M, x_rows0)
         deal_w4(1)
+        response(0, 2, "b")
+        response(0, 2, "a")
+        difference(0, 2, nc.gpsimd)
         round_w1(1, 0, 0, 4, "scalar")
         load_w2(1, "stage_z")
-        difference(0, 1)
         pair_up(0, 1, 0, M, x_rows0)
         quantize_w1(1, 0, 0)
-        response(0, 2, "a")
+        round_w1(1, 1, 0, 2, "scalar")
         response(0, 3, "b")
-        round_w1(1, 1, 0, 4, "scalar")
-        difference(0, 2)
+        response(0, 3, "a")
+        difference(0, 3, nc.gpsimd)
         pair_up(0, 2, 0, M, x_rows0)
         quantize_w1(1, 1, 0)
-        response(0, 3, "a")
+        round_w1(1, 1, 2, 2, "scalar")
         response(1, 0, "b")
-        round_w2(0)
-        difference(0, 3)
+        response(1, 0, "a")
+        difference(1, 0, nc.gpsimd)
         pair_up(0, 3, 0, M, x_rows0)
+        quantize_w1(1, 1, 2)
 
         x_rows1 = [kept([P, 4, HALF], BF16, "x_rows1%d" % u) for u in range(2)]
-        response(1, 0, "a")
-        response(1, 1, "b")
-        response(1, 1, "a")
+        for t in range(1, 4):
+            response(1, t, "b")
+            response(1, t, "a")
+            difference(1, t, nc.gpsimd)
+            pair_up(1, t - 1, 0, HALF, x_rows1[0])
         x_bf0 = interleave("scalar", x_rows0[:], M, "x_bf0")
-        difference(1, 0)
-        pair_up(1, 0, 0, HALF, x_rows1[0])
-        quantize_w2(0)
-        response(1, 2, "b")
-        response(1, 2, "a")
-        difference(1, 1)
-        pair_up(1, 1, 0, HALF, x_rows1[0])
-        x_q0 = quantize(x_bf0[:], M, "x_q0")
-        response(1, 3, "b")
-        response(1, 3, "a")
-        round_w2(1)
-        difference(1, 2)
-        pair_up(1, 2, 0, HALF, x_rows1[0])
-        difference(1, 3)
+        round_w2(0)
         pair_up(1, 3, 0, HALF, x_rows1[0])
-        quantize_w2(1)
+        x_q0 = quantize(x_bf0[:], M, "x_q0")
+        round_w2(1)
+        quantize_w2(0)
 
         y_w = kept([P, M], U32, "y_w")
         y_s = kept([P, M], U8, "y_s")
@@ -301,6 +324,7 @@ def tile_list_trawl_geometry_features_kernel(
 
         x_bf10 = interleave("scalar", x_rows1[0][:], HALF, "x_bf10")
         pair_up(1, 0, HALF, HALF, x_rows1[1])
+        quantize_w2(1)
         x_q10 = quantize(x_bf10[:], HALF, "x_q10")
         y0 = features(0, x_q10, ("scalar", "scalar"))
         y_bf0 = interleave("scalar", y0[:], HALF, "y_bf0")

@@ -75,7 +75,7 @@ def tile_list_trawl_geometry_features_kernel(
             nc.gpsimd.dma_start(low_rows[4 * b : 4 * b + 4, :].rearrange("t (m i) -> t m i", i=8), low_src[b])
         make_identity(nc, ident[:])
         for d in range(4):
-            nc.gpsimd.dma_start(
+            nc.scalar.dma_start(
                 w4s_raw[32 * d : 32 * d + 4, :, :],
                 w4_scales[:, 4 * d : 4 * d + 4, :].rearrange("a r c -> r a c").bitcast(I32),
             )
@@ -99,20 +99,23 @@ def tile_list_trawl_geometry_features_kernel(
             nc.vector.tensor_copy(words[:], tab_w[a][:].indirect(offs_t[:]))
             v_w.append(words)
 
-        w4_w, w4_s = {}, {}
+        w4_q = {}
 
-        def deal_w4(b):
-            words = kept([P, 2 * H], U8, "w4_w%d" % b)
+        def deal_w4(b, t0, count, tag=None):
+            words = kept([P, 2, count * 256], U8, "w4_w%d%d" % (b, t0), tag)
             nc.vector.tensor_copy(
-                words[:].bitcast(I32).rearrange("p (a t m e) -> p a t m e", a=2, t=4, e=4),
-                w4_raw[b][:].rearrange("p a (m t e) -> p a t m e", t=4, e=4),
+                words[:].bitcast(I32).rearrange("p a (t m e) -> p a t m e", t=count, e=4),
+                w4_raw[b][:].rearrange("p a (m t e) -> p a t m e", t=4, e=4)[:, :, t0 : t0 + count],
             )
-            scales = kept([P, H], U8, "w4_s%d" % b)
+            scales = kept([P, 2, count * P], U8, "w4_s%d%d" % (b, t0))
+            src = w4s_raw[:, :, 128 * b : 128 * b + 128].rearrange("p a (m t e) -> p a t m e", t=4, e=2)
             nc.vector.tensor_copy(
-                scales[:].bitcast(I32).rearrange("p (a t m e) -> p a t m e", a=2, t=4, e=2),
-                w4s_raw[:, :, 128 * b : 128 * b + 128].rearrange("p a (m t e) -> p a t m e", t=4, e=2),
+                scales[:].bitcast(I32).rearrange("p a (t m e) -> p a t m e", t=count, e=2),
+                src[:, :, t0 : t0 + count],
             )
-            w4_w[b], w4_s[b] = words, scales
+            for u in range(count):
+                for a in range(2):
+                    w4_q[b, a, t0 + u] = (words[:, a, 256 * u : 256 * u + 256], scales[:, a, P * u : P * u + P])
 
         def copy_on(engine, out, in_):
             if engine == "vector":
@@ -154,8 +157,8 @@ def tile_list_trawl_geometry_features_kernel(
                     codes, scales = w1_q[b, a, t]
                     lhs = codes.bitcast(FP8X4)
                 else:
-                    lhs = w4_w[b][:, 1024 * a + 256 * t : 1024 * a + 256 * t + 256].bitcast(FP4X4)
-                    scales = w4_s[b][:, 512 * a + P * t : 512 * a + P * t + P]
+                    codes, scales = w4_q[b, a, t]
+                    lhs = codes.bitcast(FP4X4)
                 nc.tensor.matmul_mx(
                     out=banks[b, t, which, half][:],
                     lhsT=lhs,
@@ -186,14 +189,18 @@ def tile_list_trawl_geometry_features_kernel(
                 engine.tensor_tensor(h[:, cols], size_a[b, t][:, cols], size_b[b, t][:, cols], ALU.subtract)
             h_t[b, t] = h
 
-        def pair_up(b, t, m0, width, x_rows):
-            port = ring.tile([P, width], F32, name="port")
-            starboard = ring.tile([P, width], F32, name="starboard")
+        def pair_up(b, t, m0, width, x_rows, after=None):
+            if after is None:
+                port = ring.tile([P, width], F32, name="port")
+                starboard = ring.tile([P, width], F32, name="starboard")
+            else:
+                starboard = kept([P, width], F32, "starboard_late%d" % t, after[0])
+                port = kept([P, width], F32, "port_late%d" % t, after[1])
             cols = slice(m0 // 16, (m0 + width) // 16)
             nc.vector.tensor_copy(starboard[:], h_t[b, t][:].indirect(pos2_t[:, cols]))
             nc.vector.tensor_copy(port[:], h_t[b, t][:].indirect(pos1_t[:, cols]))
             nc.vector.scalar_tensor_tensor(
-                x_rows[:, t, :], starboard[:], low_c[:, 4 * b + t : 4 * b + t + 1], port[:], ALU.max, ALU.add
+                x_rows[:, t, m0 : m0 + width], starboard[:], low_c[:, 4 * b + t : 4 * b + t + 1], port[:], ALU.max, ALU.add
             )
 
         def interleave(engine, rows, width, name):
@@ -228,13 +235,12 @@ def tile_list_trawl_geometry_features_kernel(
         pick_words(0)
         load_w1(0, 1, "stage_y")
         load_w4(1, "stage_w")
-        deal_w4(0)
+        deal_w4(0, 0, 1)
         one_pass(0, 0, "b", 0)
-        one_pass(0, 1, "b", 0)
         pick_words(1)
         load_w1(1, 0, "stage_z")
-        round_w1(0, 0, 0, 2, "scalar")
-        round_w1(0, 0, 2, 2, "scalar")
+        round_w1(0, 0, 0, 2, "vector")
+        round_w1(0, 0, 2, 2, "vector")
         one_pass(0, 0, "b", 1)
         take_size(0, 0, "b")
         quantize_w1(0, 0, 0)
@@ -245,51 +251,57 @@ def tile_list_trawl_geometry_features_kernel(
         quantize_w1(0, 1, 0)
         one_pass(0, 0, "a", 1)
         take_size(0, 0, "a")
+        deal_w4(0, 1, 3, "w1_bf010")
         round_w1(0, 1, 2, 2, "vector")
         quantize_w1(0, 1, 1)
         quantize_w1(0, 0, 2)
         quantize_w1(0, 1, 2)
         load_w2(0, "stage_y")
         x_rows0 = kept([P, 4, M], BF16, "x_rows0")
-        one_pass(0, 1, "b", 1)
-        take_size(0, 1, "b")
+        response(0, 1, "b")
         response(0, 1, "a")
         difference(0, 0, nc.vector)
         difference(0, 1, nc.gpsimd)
+        round_w1(1, 0, 0, 4, "scalar")
+        load_w2(1, "stage_z")
         pair_up(0, 0, 0, M, x_rows0)
-        deal_w4(1)
+        deal_w4(1, 0, 4)
         response(0, 2, "b")
         response(0, 2, "a")
         difference(0, 2, nc.gpsimd)
-        round_w1(1, 0, 0, 4, "scalar")
-        load_w2(1, "stage_z")
-        pair_up(0, 1, 0, M, x_rows0)
         quantize_w1(1, 0, 0)
         round_w1(1, 1, 0, 2, "scalar")
+        round_w1(1, 1, 2, 2, "scalar")
+        pair_up(0, 1, 0, M, x_rows0)
+        quantize_w1(1, 1, 0)
         response(0, 3, "b")
         response(0, 3, "a")
         difference(0, 3, nc.gpsimd)
         pair_up(0, 2, 0, M, x_rows0)
-        quantize_w1(1, 1, 0)
-        round_w1(1, 1, 2, 2, "scalar")
+        quantize_w1(1, 1, 2)
         response(1, 0, "b")
         response(1, 0, "a")
         difference(1, 0, nc.gpsimd)
         pair_up(0, 3, 0, M, x_rows0)
-        quantize_w1(1, 1, 2)
 
-        x_rows1 = [kept([P, 4, HALF], BF16, "x_rows1%d" % u) for u in range(2)]
-        for t in range(1, 4):
-            response(1, t, "b")
-            response(1, t, "a")
-            difference(1, t, nc.gpsimd)
-            pair_up(1, t - 1, 0, HALF, x_rows1[0])
+        x_rows1 = kept([P, 4, M], BF16, "x_rows1")
+        response(1, 1, "b")
+        response(1, 1, "a")
+        difference(1, 1, nc.gpsimd)
         x_bf0 = interleave("scalar", x_rows0[:], M, "x_bf0")
-        round_w2(0)
-        pair_up(1, 3, 0, HALF, x_rows1[0])
+        pair_up(1, 0, 0, M, x_rows1)
+        response(1, 2, "b")
+        response(1, 2, "a")
+        difference(1, 2, nc.gpsimd)
         x_q0 = quantize(x_bf0[:], M, "x_q0")
+        pair_up(1, 1, 0, M, x_rows1)
+        response(1, 3, "b")
+        response(1, 3, "a")
+        difference(1, 3, nc.gpsimd)
+        round_w2(0)
         round_w2(1)
-        quantize_w2(0)
+        pair_up(1, 2, 0, HALF, x_rows1)
+        pair_up(1, 3, 0, HALF, x_rows1)
 
         y_w = kept([P, M], U32, "y_w")
         y_s = kept([P, M], U8, "y_s")
@@ -322,18 +334,17 @@ def tile_list_trawl_geometry_features_kernel(
             nc.vector.quantize_mx(out=y_w[:, cols].bitcast(FP8X4), scales=y_s[:, cols], in_=y_bf[:])
             nc.sync.dma_start(words_out[:, cols], y_w[:, cols].bitcast(I32))
 
-        x_bf10 = interleave("scalar", x_rows1[0][:], HALF, "x_bf10")
-        pair_up(1, 0, HALF, HALF, x_rows1[1])
+        x_bf10 = interleave("scalar", x_rows1[:, :, 0:HALF], HALF, "x_bf10")
+        quantize_w2(0)
+        pair_up(1, 2, HALF, HALF, x_rows1, ("w2_bf0", None))
         quantize_w2(1)
         x_q10 = quantize(x_bf10[:], HALF, "x_q10")
         y0 = features(0, x_q10, ("scalar", "scalar"))
         y_bf0 = interleave("scalar", y0[:], HALF, "y_bf0")
-        pair_up(1, 1, HALF, HALF, x_rows1[1])
-        pair_up(1, 2, HALF, HALF, x_rows1[1])
-        pair_up(1, 3, HALF, HALF, x_rows1[1])
-        x_bf11 = interleave("vector", x_rows1[1][:], HALF, "x_bf11")
-        planes(0, y_bf0)
+        pair_up(1, 3, HALF, HALF, x_rows1, ("x_bf10", "w2_bf1"))
+        x_bf11 = interleave("vector", x_rows1[:, :, HALF:M], HALF, "x_bf11")
         x_q11 = quantize(x_bf11[:], HALF, "x_q11")
+        planes(0, y_bf0)
         y1 = features(1, x_q11, ("scalar", "vector"))
         y_bf1 = interleave("vector", y1[:], HALF, "y_bf1")
         planes(1, y_bf1)

@@ -20,6 +20,7 @@ ACT = mybir.ActivationFunctionType
 P = 128
 BANK = 512
 HALF = M // 2
+SHARE = 768
 
 
 def tile_list_trawl_geometry_features_kernel(
@@ -182,20 +183,22 @@ def tile_list_trawl_geometry_features_kernel(
 
         h_t = {}
 
-        def difference(b, t, engine):
-            h = ring.tile([P, S], F32, name="h", bufs=6)
-            for half in range(2):
-                cols = slice(BANK * half, BANK * half + BANK)
-                engine.tensor_tensor(h[:, cols], size_a[b, t][:, cols], size_b[b, t][:, cols], ALU.subtract)
-            h_t[b, t] = h
+        def difference(b, t, engine, c0, c1):
+            if (b, t) not in h_t:
+                h_t[b, t] = kept([P, S], F32, "h%d" % (4 * b + t))
+            cols = slice(c0, c1)
+            engine.tensor_tensor(h_t[b, t][:, cols], size_a[b, t][:, cols], size_b[b, t][:, cols], ALU.subtract)
 
-        def pair_up(b, t, m0, width, x_rows, after=None):
-            if after is None:
+        def pair_up(b, t, m0, width, x_rows, port_slot=None, starboard_slot=None):
+            name = "%d%d_%d" % (b, t, m0)
+            if port_slot is None:
                 port = ring.tile([P, width], F32, name="port")
+            else:
+                port = kept([P, width], F32, "port" + name, port_slot)
+            if starboard_slot is None:
                 starboard = ring.tile([P, width], F32, name="starboard")
             else:
-                starboard = kept([P, width], F32, "starboard_late%d" % t, after[0])
-                port = kept([P, width], F32, "port_late%d" % t, after[1])
+                starboard = kept([P, width], F32, "starboard" + name, starboard_slot)
             cols = slice(m0 // 16, (m0 + width) // 16)
             nc.vector.tensor_copy(starboard[:], h_t[b, t][:].indirect(pos2_t[:, cols]))
             nc.vector.tensor_copy(port[:], h_t[b, t][:].indirect(pos1_t[:, cols]))
@@ -260,47 +263,54 @@ def tile_list_trawl_geometry_features_kernel(
         x_rows0 = kept([P, 4, M], BF16, "x_rows0")
         response(0, 1, "b")
         response(0, 1, "a")
-        difference(0, 0, nc.vector)
-        difference(0, 1, nc.gpsimd)
-        round_w1(1, 0, 0, 4, "scalar")
-        load_w2(1, "stage_z")
-        pair_up(0, 0, 0, M, x_rows0)
-        deal_w4(1, 0, 4)
+        difference(0, 0, nc.vector, 0, BANK)
+        difference(0, 0, nc.vector, BANK, S)
+        pair_up(0, 0, 0, M, x_rows0, "h2")
+        difference(0, 1, nc.vector, 0, S)
         response(0, 2, "b")
         response(0, 2, "a")
-        difference(0, 2, nc.gpsimd)
-        quantize_w1(1, 0, 0)
+        difference(0, 2, nc.gpsimd, 0, SHARE)
+        round_w1(1, 0, 0, 4, "scalar")
+        load_w2(1, "stage_z")
         round_w1(1, 1, 0, 2, "scalar")
-        round_w1(1, 1, 2, 2, "scalar")
-        pair_up(0, 1, 0, M, x_rows0)
+        pair_up(0, 1, 0, M, x_rows0, "h3")
+        difference(0, 2, nc.vector, SHARE, S)
+        deal_w4(1, 0, 4)
+        quantize_w1(1, 0, 0)
         quantize_w1(1, 1, 0)
         response(0, 3, "b")
         response(0, 3, "a")
-        difference(0, 3, nc.gpsimd)
-        pair_up(0, 2, 0, M, x_rows0)
+        difference(0, 3, nc.gpsimd, 0, SHARE)
+        round_w1(1, 1, 2, 2, "scalar")
+        pair_up(0, 2, 0, M, x_rows0, "h4")
+        difference(0, 3, nc.vector, SHARE, S)
         quantize_w1(1, 1, 2)
         response(1, 0, "b")
         response(1, 0, "a")
-        difference(1, 0, nc.gpsimd)
-        pair_up(0, 3, 0, M, x_rows0)
+        difference(1, 0, nc.gpsimd, 0, SHARE)
+        pair_up(0, 3, 0, M, x_rows0, "h5")
+        difference(1, 0, nc.vector, SHARE, S)
 
         x_rows1 = kept([P, 4, M], BF16, "x_rows1")
         response(1, 1, "b")
         response(1, 1, "a")
-        difference(1, 1, nc.gpsimd)
+        difference(1, 1, nc.gpsimd, 0, SHARE)
         x_bf0 = interleave("scalar", x_rows0[:], M, "x_bf0")
-        pair_up(1, 0, 0, M, x_rows1)
+        pair_up(1, 0, 0, M, x_rows1, "h6")
+        difference(1, 1, nc.vector, SHARE, S)
         response(1, 2, "b")
         response(1, 2, "a")
-        difference(1, 2, nc.gpsimd)
+        difference(1, 2, nc.gpsimd, 0, SHARE)
         x_q0 = quantize(x_bf0[:], M, "x_q0")
-        pair_up(1, 1, 0, M, x_rows1)
+        pair_up(1, 1, 0, M, x_rows1, "h7")
+        difference(1, 2, nc.vector, SHARE, S)
         response(1, 3, "b")
         response(1, 3, "a")
-        difference(1, 3, nc.gpsimd)
+        difference(1, 3, nc.gpsimd, 0, BANK)
         round_w2(0)
         round_w2(1)
         pair_up(1, 2, 0, HALF, x_rows1)
+        difference(1, 3, nc.vector, BANK, S)
         pair_up(1, 3, 0, HALF, x_rows1)
 
         y_w = kept([P, M], U32, "y_w")
@@ -336,12 +346,12 @@ def tile_list_trawl_geometry_features_kernel(
 
         x_bf10 = interleave("scalar", x_rows1[:, :, 0:HALF], HALF, "x_bf10")
         quantize_w2(0)
-        pair_up(1, 2, HALF, HALF, x_rows1, ("w2_bf0", None))
+        pair_up(1, 2, HALF, HALF, x_rows1, None, "w2_bf0")
         quantize_w2(1)
         x_q10 = quantize(x_bf10[:], HALF, "x_q10")
         y0 = features(0, x_q10, ("scalar", "scalar"))
         y_bf0 = interleave("scalar", y0[:], HALF, "y_bf0")
-        pair_up(1, 3, HALF, HALF, x_rows1, ("x_bf10", "w2_bf1"))
+        pair_up(1, 3, HALF, HALF, x_rows1, "w2_bf1", "x_bf10")
         x_bf11 = interleave("vector", x_rows1[:, :, HALF:M], HALF, "x_bf11")
         x_q11 = quantize(x_bf11[:], HALF, "x_q11")
         planes(0, y_bf0)

from contextlib import ExitStack

import concourse.mybir as mybir
from concourse.masks import make_identity

K, H, N, T, S, M = 1024, 1024, 512, 2048, 1024, 512
FLOPS = 2 * 2 * K * H * S + 2 * H * N * M

F32 = mybir.dt.float32
BF16 = mybir.dt.bfloat16
I32 = mybir.dt.int32
U32 = mybir.dt.uint32
U16 = mybir.dt.uint16
U8 = mybir.dt.uint8
FP8X4 = mybir.dt.float8_e4m3fn_x4
FP4X4 = mybir.dt.float4_e2m1fn_x4
ALU = mybir.AluOpType
ACT = mybir.ActivationFunctionType

P = 128
BANK = 512
HALF = M // 2
SHARE = 768


def tile_list_trawl_geometry_features_kernel(
    tc, tab_words, tab_scales, offs, pos1, pos2, w1, w4_words, w4_scales, low, w2, out_0, out_1, out_2
):
    nc = tc.nc
    with ExitStack() as ctx:
        keep = ctx.enter_context(tc.tile_pool(name="keep", bufs=1))
        ring = ctx.enter_context(tc.tile_pool(name="ring", bufs=2))
        psum = ctx.enter_context(tc.psum_pool(name="psum", bufs=4))

        def kept(shape, dtype, name, tag=None):
            return keep.tile(shape, dtype, name=name, tag=tag or name, align_bytes=64)

        offs_t = kept([P, S // 16], U16, "offs_t")
        pos1_t = kept([P, M // 16], U16, "pos1_t")
        pos2_t = kept([P, M // 16], U16, "pos2_t")
        tab_s = kept([P, T], U8, "tab_s", "stage_x")
        tab_w = [kept([P, T], U32, "tab_w0", "stage_y"), kept([P, T], U32, "tab_w1", "stage_z")]
        w4s_raw = kept([P, 2, H // 4], I32, "w4s_raw")
        v_s = kept([P, 2 * S], U8, "v_s")
        low_rows = kept([P, P], F32, "low_rows")
        ident = kept([P, P], F32, "ident")

        nc.gpsimd.memset(tab_s[:].bitcast(I32), 0)
        nc.gpsimd.memset(low_rows[:], 0.0)
        nc.vector.memset(w4s_raw[:], 0)
        nc.vector.memset(v_s[:].bitcast(I32), 0)

        nc.sync.dma_start(offs_t[:], offs)
        nc.sync.dma_start(pos1_t[:], pos1)
        nc.sync.dma_start(pos2_t[:], pos2)
        nc.sync.dma_start(tab_s[0:P:4, :].bitcast(I32), tab_scales.rearrange("a q t -> q a t").bitcast(I32))
        nc.sync.dma_start(tab_w[0][:].bitcast(I32), tab_words[0].rearrange("p t i -> p (t i)").bitcast(I32))
        w4_raw, w1_raw = {}, {}

        def load_w4(b, tag):
            raw = kept([P, 2, H // 4], I32, "w4_raw%d" % b, tag)
            src = w4_words.rearrange("a p c -> p a c")[:, :, 1024 * b : 1024 * b + 1024]
            nc.sync.dma_start(raw[:], src.bitcast(I32))
            w4_raw[b] = raw

        def load_w1(b, a, tag):
            raw = kept([P, 4, BANK], F32, "w1_raw%d%d" % (b, a), tag)
            rows = w1[512 * a : 512 * a + 512, 512 * b : 512 * b + 512]
            nc.sync.dma_start(raw[:], rows.rearrange("(p j) c -> p j c", j=4))
            w1_raw[b, a] = raw

        load_w4(0, "w4_raw0")
        nc.sync.dma_start(tab_w[1][:].bitcast(I32), tab_words[1].rearrange("p t i -> p (t i)").bitcast(I32))
        low_src = low.rearrange("(b m t i) -> b t m i", b=2, t=4, i=8)
        for b in range(2):
            nc.gpsimd.dma_start(low_rows[4 * b : 4 * b + 4, :].rearrange("t (m i) -> t m i", i=8), low_src[b])
        make_identity(nc, ident[:])
        for d in range(4):
            nc.scalar.dma_start(
                w4s_raw[32 * d : 32 * d + 4, :, :],
                w4_scales[:, 4 * d : 4 * d + 4, :].rearrange("a r c -> r a c").bitcast(I32),
            )
        low_ps = psum.tile([P, BANK], F32, name="low_ps", tag="bank_a")
        nc.tensor.transpose(low_ps[:, 0:P], low_rows[:], ident[:])
        low_c = kept([P, 8], F32, "low_c")
        nc.scalar.activation(low_c[:], low_ps[:, 0:8], ACT.Copy)

        picked_s = kept([P, S], U8, "picked_s", "stage_w")
        nc.vector.tensor_copy(picked_s[:], tab_s[:].indirect(offs_t[:]))
        for d in range(4):
            nc.sync.dma_start(
                v_s[32 * d : 32 * d + 4, :].bitcast(I32).rearrange("r (a c) -> r a c", a=2),
                picked_s[32 * d : 32 * d + 32 : 4, :].bitcast(I32),
            )
        load_w1(0, 0, "stage_x")
        v_w = []

        def pick_words(a):
            words = kept([P, S], U32, "v_w%d" % a)
            nc.vector.tensor_copy(words[:], tab_w[a][:].indirect(offs_t[:]))
            v_w.append(words)

        w4_q = {}

        def deal_w4(b, t0, count, tag=None):
            words = kept([P, 2, count * 256], U8, "w4_w%d%d" % (b, t0), tag)
            nc.vector.tensor_copy(
                words[:].bitcast(I32).rearrange("p a (t m e) -> p a t m e", t=count, e=4),
                w4_raw[b][:].rearrange("p a (m t e) -> p a t m e", t=4, e=4)[:, :, t0 : t0 + count],
            )
            scales = kept([P, 2, count * P], U8, "w4_s%d%d" % (b, t0))
            src = w4s_raw[:, :, 128 * b : 128 * b + 128].rearrange("p a (m t e) -> p a t m e", t=4, e=2)
            nc.vector.tensor_copy(
                scales[:].bitcast(I32).rearrange("p a (t m e) -> p a t m e", t=count, e=2),
                src[:, :, t0 : t0 + count],
            )
            for u in range(count):
                for a in range(2):
                    w4_q[b, a, t0 + u] = (words[:, a, 256 * u : 256 * u + 256], scales[:, a, P * u : P * u + P])

        def copy_on(engine, out, in_):
            if engine == "vector":
                nc.vector.tensor_copy(out, in_)
            else:
                nc.scalar.copy(out, in_)

        w1_bf, w1_q = {}, {}

        def round_w1(b, a, t0, count, engine):
            tile_ = kept([P, count * 512], BF16, "w1_bf%d%d%d" % (b, a, t0))
            src = w1_raw[b, a][:].rearrange("p j (m t h l) -> p t m h j l", t=4, h=2, l=4)
            for u in range(count):
                dst = tile_[:, 512 * u : 512 * u + 512].rearrange("p (m h l j) -> p m h j l", h=2, l=4, j=4)
                copy_on(engine, dst, src[:, t0 + u])
            w1_bf[b, a, t0] = (tile_, count)

        def quantize(src, width, name):
            codes = kept([P, width], U32, name + "_w")
            scales = kept([P, width], U8, name + "_s")
            nc.vector.quantize_mx(out=codes[:].bitcast(FP8X4), scales=scales[:], in_=src)
            return codes, scales

        def quantize_w1(b, a, t0):
            tile_, count = w1_bf[b, a, t0]
            codes, scales = quantize(tile_[:], count * P, "w1_q%d%d%d" % (b, a, t0))
            for u in range(count):
                w1_q[b, a, t0 + u] = (codes[:, P * u : P * u + P], scales[:, P * u : P * u + P])

        size_a, size_b = {}, {}

        banks = {}

        def one_pass(b, t, which, a):
            for half in range(2):
                if a == 0:
                    banks[b, t, which, half] = psum.tile([P, BANK], F32, name="acc", tag="bank_" + which)
                if which == "a":
                    codes, scales = w1_q[b, a, t]
                    lhs = codes.bitcast(FP8X4)
                else:
                    codes, scales = w4_q[b, a, t]
                    lhs = codes.bitcast(FP4X4)
                nc.tensor.matmul_mx(
                    out=banks[b, t, which, half][:],
                    lhsT=lhs,
                    lhsT_scale=scales,
                    rhs=v_w[a][:, BANK * half : BANK * half + BANK].bitcast(FP8X4),
                    rhs_scale=v_s[:, S * a + BANK * half : S * a + BANK * half + BANK],
                    start=(a == 0),
                    stop=(a == 1),
                )

        def take_size(b, t, which):
            size = ring.tile([P, S], F32, name="size_" + which, bufs=3)
            for half in range(2):
                nc.scalar.activation(size[:, BANK * half : BANK * half + BANK], banks[b, t, which, half][:], ACT.Abs)
            (size_a if which == "a" else size_b)[b, t] = size

        def response(b, t, which):
            one_pass(b, t, which, 0)
            one_pass(b, t, which, 1)
            take_size(b, t, which)

        h_t = {}

        def difference(b, t, engine, c0, c1):
            if (b, t) not in h_t:
                h_t[b, t] = kept([P, S], F32, "h%d" % (4 * b + t))
            cols = slice(c0, c1)
            engine.tensor_tensor(h_t[b, t][:, cols], size_a[b, t][:, cols], size_b[b, t][:, cols], ALU.subtract)

        def pair_up(b, t, m0, width, x_rows, port_slot=None, starboard_slot=None):
            name = "%d%d_%d" % (b, t, m0)
            if port_slot is None:
                port = ring.tile([P, width], F32, name="port")
            else:
                port = kept([P, width], F32, "port" + name, port_slot)
            if starboard_slot is None:
                starboard = ring.tile([P, width], F32, name="starboard")
            else:
                starboard = kept([P, width], F32, "starboard" + name, starboard_slot)
            cols = slice(m0 // 16, (m0 + width) // 16)
            nc.vector.tensor_copy(starboard[:], h_t[b, t][:].indirect(pos2_t[:, cols]))
            nc.vector.tensor_copy(port[:], h_t[b, t][:].indirect(pos1_t[:, cols]))
            nc.vector.scalar_tensor_tensor(
                x_rows[:, t, m0 : m0 + width], starboard[:], low_c[:, 4 * b + t : 4 * b + t + 1], port[:], ALU.max, ALU.add
            )

        def interleave(engine, rows, width, name):
            woven = kept([P, 4 * width], BF16, name)
            copy_on(
                engine,
                woven[:].rearrange("p (c l t) -> p c t l", l=4, t=4),
                rows.rearrange("p t (c l) -> p c t l", l=4),
            )
            return woven

        w2_raw, w2_bf, w2_q = {}, {}, {}

        def load_w2(b, tag):
            raw = kept([P, 4, N], F32, "w2_raw%d" % b, tag)
            src = w2[512 * b : 512 * b + 512, :].rearrange("(m t i) n -> t m i n", t=4, i=8)
            for t in range(4):
                nc.sync.dma_start(raw[:, t, :], src[t])
            w2_raw[b] = raw

        def round_w2(b):
            tile_ = kept([P, 4 * N], BF16, "w2_bf%d" % b)
            dst = tile_[:].rearrange("p (s q t) -> p q t s", s=4, t=4)
            src = w2_raw[b][:].rearrange("p t (q s) -> p q t s", s=4)
            for u in range(4):
                nc.scalar.copy(dst[:, 32 * u : 32 * u + 32], src[:, 32 * u : 32 * u + 32])
            w2_bf[b] = tile_

        def quantize_w2(b):
            w2_q[b] = quantize(w2_bf[b][:], N, "w2_q%d" % b)

        pick_words(0)
        load_w1(0, 1, "stage_y")
        load_w4(1, "stage_w")
        deal_w4(0, 0, 1)
        one_pass(0, 0, "b", 0)
        pick_words(1)
        load_w1(1, 0, "stage_z")
        round_w1(0, 0, 0, 2, "vector")
        round_w1(0, 0, 2, 2, "vector")
        one_pass(0, 0, "b", 1)
        take_size(0, 0, "b")
        quantize_w1(0, 0, 0)
        one_pass(0, 0, "a", 0)
        load_w1(1, 1, "stage_x")
        round_w1(0, 1, 0, 1, "vector")
        round_w1(0, 1, 1, 1, "vector")
        quantize_w1(0, 1, 0)
        one_pass(0, 0, "a", 1)
        take_size(0, 0, "a")
        deal_w4(0, 1, 3, "w1_bf010")
        round_w1(0, 1, 2, 2, "vector")
        quantize_w1(0, 1, 1)
        quantize_w1(0, 0, 2)
        quantize_w1(0, 1, 2)
        load_w2(0, "stage_y")
        x_rows0 = kept([P, 4, M], BF16, "x_rows0")
        response(0, 1, "b")
        response(0, 1, "a")
        difference(0, 0, nc.vector, 0, BANK)
        difference(0, 0, nc.vector, BANK, S)
        pair_up(0, 0, 0, M, x_rows0, "h2")
        difference(0, 1, nc.vector, 0, S)
        response(0, 2, "b")
        response(0, 2, "a")
        difference(0, 2, nc.gpsimd, 0, SHARE)
        round_w1(1, 0, 0, 4, "scalar")
        load_w2(1, "stage_z")
        round_w1(1, 1, 0, 2, "scalar")
        pair_up(0, 1, 0, M, x_rows0, "h3")
        difference(0, 2, nc.vector, SHARE, S)
        deal_w4(1, 0, 4)
        quantize_w1(1, 0, 0)
        quantize_w1(1, 1, 0)
        response(0, 3, "b")
        response(0, 3, "a")
        difference(0, 3, nc.gpsimd, 0, SHARE)
        round_w1(1, 1, 2, 2, "scalar")
        pair_up(0, 2, 0, M, x_rows0, "h4")
        difference(0, 3, nc.vector, SHARE, S)
        quantize_w1(1, 1, 2)
        response(1, 0, "b")
        response(1, 0, "a")
        difference(1, 0, nc.gpsimd, 0, SHARE)
        pair_up(0, 3, 0, M, x_rows0, "h5")
        difference(1, 0, nc.vector, SHARE, S)

        x_rows1 = kept([P, 4, M], BF16, "x_rows1")
        response(1, 1, "b")
        response(1, 1, "a")
        difference(1, 1, nc.gpsimd, 0, SHARE)
        x_bf0 = interleave("scalar", x_rows0[:], M, "x_bf0")
        pair_up(1, 0, 0, M, x_rows1, "h6")
        difference(1, 1, nc.vector, SHARE, S)
        response(1, 2, "b")
        response(1, 2, "a")
        difference(1, 2, nc.gpsimd, 0, SHARE)
        x_q0 = quantize(x_bf0[:], M, "x_q0")
        pair_up(1, 1, 0, M, x_rows1, "h7")
        difference(1, 2, nc.vector, SHARE, S)
        response(1, 3, "b")
        response(1, 3, "a")
        difference(1, 3, nc.gpsimd, 0, BANK)
        round_w2(0)
        round_w2(1)
        pair_up(1, 2, 0, HALF, x_rows1)
        difference(1, 3, nc.vector, BANK, S)
        pair_up(1, 3, 0, HALF, x_rows1)

        y_w = kept([P, M], U32, "y_w")
        y_s = kept([P, M], U8, "y_s")
        y_out = out_0.rearrange("(q s) m -> q s m", s=4)
        words_out = out_1[0].rearrange("p m t -> p (m t)").bitcast(I32)

        def features(u, x_q1, engines):
            cols = slice(HALF * u, HALF * u + HALF)
            y = kept([P, 4, HALF], F32, "y%d" % u)
            for s in range(4):
                acc = psum.tile([P, BANK], F32, name="acc", tag="bank_a" if u == 0 else "bank_b")
                for b in range(2):
                    codes, scales = w2_q[b]
                    x_w, x_s = (x_q0[0][:, cols], x_q0[1][:, cols]) if b == 0 else (x_q1[0][:], x_q1[1][:])
                    nc.tensor.matmul_mx(
                        out=acc[:, 0:HALF],
                        lhsT=codes[:, P * s : P * s + P].bitcast(FP8X4),
                        lhsT_scale=scales[:, P * s : P * s + P],
                        rhs=x_w.bitcast(FP8X4),
                        rhs_scale=x_s,
                        start=(b == 0),
                        stop=(b == 1),
                    )
                copy_on(engines[s % 2], y[:, s, :], acc[:, 0:HALF])
            nc.sync.dma_start(y_out[:, :, cols], y[:])
            return y

        def planes(u, y_bf):
            cols = slice(HALF * u, HALF * u + HALF)
            nc.vector.quantize_mx(out=y_w[:, cols].bitcast(FP8X4), scales=y_s[:, cols], in_=y_bf[:])
            nc.sync.dma_start(words_out[:, cols], y_w[:, cols].bitcast(I32))

        x_bf10 = interleave("scalar", x_rows1[:, :, 0:HALF], HALF, "x_bf10")
        quantize_w2(0)
        pair_up(1, 2, HALF, HALF, x_rows1, None, "w2_bf0")
        quantize_w2(1)
        x_q10 = quantize(x_bf10[:], HALF, "x_q10")
        y0 = features(0, x_q10, ("scalar", "scalar"))
        y_bf0 = interleave("scalar", y0[:], HALF, "y_bf0")
        pair_up(1, 3, HALF, HALF, x_rows1, "w2_bf1", "x_bf10")
        x_bf11 = interleave("vector", x_rows1[:, :, HALF:M], HALF, "x_bf11")
        x_q11 = quantize(x_bf11[:], HALF, "x_q11")
        planes(0, y_bf0)
        y1 = features(1, x_q11, ("scalar", "vector"))
        y_bf1 = interleave("vector", y1[:], HALF, "y_bf1")
        planes(1, y_bf1)
        for d in range(4):
            queue = nc.scalar if d % 2 else nc.sync
            queue.dma_start(out_2[0, 4 * d : 4 * d + 4, :].bitcast(I32), y_s[32 * d : 32 * d + 4, :].bitcast(I32))
